import numpy as np
CORES = [64,65,66,67,68,69,70,71,72,73,74,75,76,77,78,79,80,81,82,83,84,85,86,87,88,89,90,91,92,93,94,95]
N = 32
T, K = 4, 4
ROUTE = [[[21,13,23,1],[31,26,10,18],[7,9,17,19],[27,4,8,5]],[[30,16,22,27],[4,29,21,0],[25,24,7,11],[24,31,26,1]],[[2,7,3,8],[7,29,0,15],[8,11,4,3],[11,10,17,29]],[[1,10,6,23],[21,29,0,9],[16,1,7,6],[7,3,27,10]],[[30,23,4,3],[2,11,7,22],[14,25,23,2],[6,13,18,10]],[[20,28,17,0],[25,7,14,30],[9,31,2,25],[1,4,5,8]],[[12,16,19,6],[4,23,27,3],[19,5,21,15],[26,16,2,20]],[[27,22,19,10],[5,19,10,4],[7,6,29,19],[14,5,6,15]],[[31,26,1,10],[20,15,18,0],[16,14,4,7],[5,2,13,24]],[[21,19,27,13],[17,31,15,4],[25,31,30,1],[3,31,29,27]],[[26,13,24,25],[29,4,11,17],[9,29,20,11],[8,14,11,30]],[[20,23,17,30],[20,31,27,8],[27,4,8,24],[22,2,5,1]],[[19,6,22,27],[25,31,22,21],[21,18,25,20],[10,13,0,23]],[[28,29,15,9],[21,13,4,16],[7,30,9,22],[8,1,26,22]],[[1,8,6,19],[6,1,18,23],[14,1,16,27],[15,0,12,8]],[[4,9,12,0],[17,19,4,20],[27,11,12,9],[11,10,30,16]],[[20,4,8,14],[10,14,18,28],[12,18,27,8],[17,30,25,8]],[[24,22,17,31],[17,4,20,28],[6,19,26,11],[19,31,25,12]],[[13,14,1,18],[26,28,31,0],[14,13,8,11],[23,8,31,18]],[[11,14,27,22],[11,18,23,16],[29,20,7,30],[13,14,3,11]],[[24,30,4,0],[14,24,15,12],[28,25,23,22],[22,2,11,13]],[[1,13,28,19],[29,30,9,22],[23,14,19,10],[7,21,29,12]],[[15,31,7,26],[28,10,1,22],[25,23,5,18],[9,0,27,4]],[[21,12,17,16],[26,30,6,20],[2,28,13,15],[26,8,31,21]],[[18,24,30,27],[18,0,6,25],[26,5,18,16],[20,18,21,12]],[[6,14,21,12],[1,12,2,18],[19,11,26,15],[19,31,6,13]],[[5,12,3,13],[25,18,15,6],[1,25,17,19],[28,12,17,25]],[[17,22,9,25],[8,17,27,5],[9,31,26,25],[7,24,18,20]],[[2,28,24,12],[3,2,26,1],[30,24,7,14],[11,19,31,28]],[[27,21,12,18],[28,14,0,22],[4,31,25,21],[9,0,31,20]],[[9,16,20,8],[13,23,26,20],[13,4,16,1],[14,29,13,9]],[[6,16,3,21],[18,24,13,28],[23,15,0,1],[16,9,21,4]]]
ZW = 21
def setup_inputs(rng):
    return {"z": rng.standard_normal((N, 128, ZW), dtype=np.float32), "g": rng.random((N, 128, T * K), dtype=np.float32)}
def reference(z, g):
    y = np.zeros((N, 128, T), np.float64)
    fill = [0] * N
    for r in range(N):
        for t in range(T):
            for k, e in enumerate(ROUTE[r][t]):
                y[r][:, t] += g[r][:, t * K + k].astype(np.float64) * z[e][:, fill[e]].astype(np.float64)
                fill[e] += 1
    return {"y": y.astype(z.dtype)}

@@ -1,0 +1,103 @@
+from concourse.mybir import AluOpType
+
+SCRATCH = {
+    "zs": ("sbuf", [128, 21], "float32"),
+    "rz": ("sbuf", [128, 21], "float32"),
+    "gs": ("sbuf", [128, 16], "float32"),
+    "land": ("sbuf", [128, 16], "float32"),
+    "prod": ("sbuf", [128, 16], "float32"),
+    "half": ("sbuf", [128, 8], "float32"),
+    "ys": ("sbuf", [128, 4], "float32"),
+}
+SEMAPHORES = ["zl", "gl", "arrived", "relay", "sent", "vs", "stored"]
+
+
+def rank_program(g, core, T, topo):
+    me = T.rank_of(core)
+    if me is None:
+        return
+    cores = T.cores
+    n = len(cores)
+    route = T.tables["ROUTE"]
+    nt, nk = T.tables["T"], T.tables["K"]
+    col = [[] for _ in range(n)]
+    for r in range(n):
+        for t in range(nt):
+            for k in range(nk):
+                col[route[r][t][k]].append((r, t, k))
+
+    def block(e, r):
+        idx = [i for i, it in enumerate(col[e]) if it[0] == r]
+        return (idx[0], len(idx)) if idx else (0, 0)
+
+    def slot(r, e):
+        return sum(block(x, r)[1] for x in range(e) if x != r)
+
+    def carrier(e, r):
+        if topo.may_write(cores[e], cores[r]):
+            return cores[e]
+        return cores[e] + 2
+
+    def nbits(m):
+        return bin(m).count("1")
+
+    g.sync.dma_start(T.zs[:], T.z[:]).then_inc(T.sem.zl, 16)
+    g.scalar.dma_start(T.gs[:], T.g[:]).then_inc(T.sem.gl, 16)
+
+    sent = 0
+    g.wait_ge(T.sem.zl, 16)
+    needs_relay = any(block(me, r)[1] and carrier(me, r) != core for r in range(n) if r != me)
+    if needs_relay:
+        rid, pid, _ = topo.addr(core + 2)
+        m = topo.mask(core, core + 2)
+        g.remote_dma(T.rz[:], T.zs[:], T.sem.relay, T.sem.sent, pid, rid, m)
+        sent += nbits(m)
+    for r in range(n):
+        o, c = block(me, r)
+        if r == me or not c or carrier(me, r) != core:
+            continue
+        rid, pid, _ = topo.addr(cores[r])
+        m = topo.mask(core, cores[r])
+        s = slot(r, me)
+        g.remote_dma(T.land[:, s:s + c], T.zs[:, o:o + c], T.sem.arrived, T.sem.sent, pid, rid, m)
+        sent += nbits(m)
+    if core % 4 >= 2:
+        e = me - 2
+        fw = [r for r in range(n) if block(e, r)[1] and carrier(e, r) == core]
+        if fw:
+            g.wait_ge(T.sem.relay, 16)
+        for r in fw:
+            o, c = block(e, r)
+            rid, pid, _ = topo.addr(cores[r])
+            m = topo.mask(core, cores[r])
+            s = slot(r, e)
+            g.remote_dma(T.land[:, s:s + c], T.rz[:, o:o + c], T.sem.arrived, T.sem.sent, pid, rid, m)
+            sent += nbits(m)
+    g.wait_ge(T.sem.sent, sent)
+
+    expect = 0
+    for e in range(n):
+        if e != me and block(e, me)[1]:
+            expect += nbits(topo.mask(carrier(e, me), core))
+    v = g.vector
+    v.wait_ge(T.sem.gl, 16)
+    v.wait_ge(T.sem.zl, 16)
+    v.wait_ge(T.sem.arrived, expect)
+    for t in range(nt):
+        for k in range(nk):
+            e = route[me][t][k]
+            i = col[e].index((me, t, k))
+            if e == me:
+                src = T.zs[:, i:i + 1]
+            else:
+                p = slot(me, e) + i - block(e, me)[0]
+                src = T.land[:, p:p + 1]
+            q = k * nt + t
+            v.tensor_tensor(T.prod[:, q:q + 1], T.gs[:, t * nk + k:t * nk + k + 1], src, AluOpType.mult).then_inc(T.sem.vs, 1)
+    v.wait_ge(T.sem.vs, 16)
+    v.tensor_tensor(T.half[:], T.prod[:, 0:8], T.prod[:, 8:16], AluOpType.add).then_inc(T.sem.vs, 1)
+    v.wait_ge(T.sem.vs, 17)
+    v.tensor_tensor(T.ys[:], T.half[:, 0:4], T.half[:, 4:8], AluOpType.add).then_inc(T.sem.vs, 1)
+    g.sync.wait_ge(T.sem.vs, 18)
+    g.sync.dma_start(T.y[:], T.ys[:]).then_inc(T.sem.stored, 16)
+    g.sync.wait_ge(T.sem.stored, 16)

@@ -1,103 +1,231 @@
+from concourse.bass import DstId, RemoteDMATransfer
 from concourse.mybir import AluOpType
 
+RMAX = 32
 SCRATCH = {
-    "zs": ("sbuf", [128, 21], "float32"),
-    "rz": ("sbuf", [128, 21], "float32"),
-    "gs": ("sbuf", [128, 16], "float32"),
-    "land": ("sbuf", [128, 16], "float32"),
-    "prod": ("sbuf", [128, 16], "float32"),
-    "half": ("sbuf", [128, 8], "float32"),
-    "ys": ("sbuf", [128, 4], "float32"),
+    "z3": ("sbuf", [16, 168], "float32"),
+    "g3": ("sbuf", [16, 8, 16], "float32"),
+    "gp": ("sbuf", [16, 8, 16], "float32"),
+    "seed": ("sbuf", [128, 80], "float32"),
+    "cst": ("sbuf", [16, 20], "float32"),
+    "zT": ("sbuf", [21, 128], "float32"),
+    "lt": ("sbuf", [16, 128], "float32"),
+    "prod": ("sbuf", [16, 128], "float32"),
+    "own": ("sbuf", [16, 32], "float32"),
+    "y3": ("sbuf", [16, 32], "float32"),
+    "zd": ("dram", [21, 128, 1], "float32"),
+    "land": ("dram", [16, 128, 1], "float32"),
+    "rl": ("dram", [RMAX, 128, 1], "float32"),
+    "pc": ("psum", [128, 512], "float32"),
+    "pz": ("psum", [128, 512], "float32"),
+    "pg": ("psum", [128, 512], "float32"),
+    "py": ("psum", [128, 512], "float32"),
 }
-SEMAPHORES = ["zl", "gl", "arrived", "relay", "sent", "vs", "stored"]
+SEMAPHORES = ["zl", "gl", "cs", "cm", "cc", "zm", "zc", "zs", "gv", "gm", "arrived", "relay", "sent", "ll", "pm", "ym",
+              "yc", "st"]
+
+CACHE = {}
+
+
+def links(topo, s, d):
+    a, b = topo.chip(s), topo.chip(d)
+    out = [("w", s), ("l", d)]
+    if a != b:
+        dd = topo.die(s)
+        out += [("out", a), ("in", b)]
+        if (a & 1) != (b & 1):
+            out.append(("mate", a, dd))
+            a ^= 1
+        if a != b:
+            out += [("so", a, dd), ("si", b, dd)]
+    return out
+
+
+def plan(T, topo):
+    if "plan" in CACHE:
+        return CACHE["plan"]
+    cores = T.cores
+    route = T.tables["ROUTE"]
+    fill = [0] * len(cores)
+    raw = []
+    for r, toks in enumerate(route):
+        slot = 0
+        for t, exps in enumerate(toks):
+            for k, e in enumerate(exps):
+                raw.append([cores[e], fill[e], cores[r], None if e == r else slot, None, None, t, k])
+                fill[e] += 1
+                slot += e != r
+
+    ncore = (max(cores) // 8 + 1) * 8
+    pw = [n ** 6 for n in range(len(raw) * 2 + 2)]
+    weight = {"w": 4096, "l": 4096, "mate": 4096, "so": 4096, "si": 4096, "out": 1, "in": 1}
+    load = {}
+
+    def way(it, q):
+        return links(topo, it[0], it[2]) if q is None else links(topo, it[0], q) + links(topo, q, it[2])
+
+    def put(ks, sign):
+        cost = 0
+        for key in ks:
+            n = load.get(key, 0)
+            cost += weight[key[0]] * (pw[n + sign] - pw[n])
+            load[key] = n + sign
+        return cost
+
+    ways = []
+    for it in raw:
+        src, dst = it[0], it[2]
+        if src == dst:
+            ways.append([])
+            continue
+        opts = [None] if topo.may_write(src, dst) else []
+        if (topo.chip(src) & 1) != (topo.chip(dst) & 1):
+            opts += [q for q in range(ncore) if q != src and (topo.chip(q) & 1) == (topo.chip(src) & 1)
+                     and topo.may_write(q, dst)]
+        ways.append([(q, way(it, q)) for q in opts])
+    chosen = [None] * len(raw)
+    for sweep in range(16):
+        moved = False
+        for i, opts in enumerate(ways):
+            if not opts or (sweep and len(opts) < 2):
+                continue
+            if chosen[i] is not None:
+                put(chosen[i][1], -1)
+            best = None
+            for o in opts:
+                cost = put(o[1], 1)
+                put(o[1], -1)
+                if best is None or cost < best[0]:
+                    best = (cost, o)
+            moved = moved or best[1] is not chosen[i]
+            chosen[i] = best[1]
+            put(best[1][1], 1)
+        if not moved:
+            break
+
+    res = {"src": {}, "via": {}, "dst": {}}
+    for it, ch in zip(raw, chosen):
+        if ch is not None and ch[0] is not None:
+            it[4] = ch[0]
+            it[5] = len(res["via"].setdefault(ch[0], []))
+            assert it[5] < RMAX
+            res["via"][ch[0]].append(it)
+        res["src"].setdefault(it[0], []).append(it)
+        res["dst"].setdefault(it[2], []).append(it)
+    CACHE["plan"] = res
+    return res
 
 
 def rank_program(g, core, T, topo):
-    me = T.rank_of(core)
-    if me is None:
+    routes = plan(T, topo)
+    sem = T.sem
+    thru = routes["via"].get(core, [])
+    nsent = [0]
+
+    def emit(writes):
+        todo = list(writes)
+        while todo:
+            far = [w for w in todo if topo.chip(w[0]) != topo.chip(core)][:8]
+            near = [w for w in todo if topo.chip(w[0]) == topo.chip(core)][:16 - len(far)]
+            call = []
+            for eng, w in enumerate(far + near):
+                rid, pid, _ = topo.addr(w[0])
+                call.append(RemoteDMATransfer(dst_ids=[DstId(rid=rid, pnc=pid)], dma_engine_mask=1 << eng,
+                                              remote_sem=w[3], src=w[2], dst=w[1]))
+                todo.remove(w)
+            g.remote_dma_fused(call, local_sem=sem.sent)
+            nsent[0] += len(call)
+
+    def pass_on():
+        if thru:
+            g.wait_ge(sem.relay, len(thru))
+            emit([(it[2], T.land[it[3]], T.rl[it[5]], sem.arrived) for it in thru])
+        if nsent[0]:
+            g.wait_ge(sem.sent, nsent[0])
+
+    if T.rank_of(core) is None:
+        pass_on()
         return
-    cores = T.cores
-    n = len(cores)
-    route = T.tables["ROUTE"]
-    nt, nk = T.tables["T"], T.tables["K"]
-    col = [[] for _ in range(n)]
-    for r in range(n):
-        for t in range(nt):
-            for k in range(nk):
-                col[route[r][t][k]].append((r, t, k))
 
-    def block(e, r):
-        idx = [i for i, it in enumerate(col[e]) if it[0] == r]
-        return (idx[0], len(idx)) if idx else (0, 0)
+    nt, nk, zw = T.tables["T"], T.tables["K"], T.tables["ZW"]
+    assert nt == 4 and nk == 4 and zw == 21
+    v, pe, sy, sc = g.vector, g.tensor, g.sync, g.scalar
+    mine = routes["src"].get(core, [])
+    wanted = routes["dst"][core]
+    own = [it for it in wanted if it[3] is None]
+    nz, nrem = len(mine), len(wanted) - len(own)
 
-    def slot(r, e):
-        return sum(block(x, r)[1] for x in range(e) if x != r)
+    sy.dma_start(T.z3[:], T.z[:]).then_inc(sem.zl, 16)
+    sc.dma_start(T.g3[:], T.g[:]).then_inc(sem.gl, 16)
 
-    def carrier(e, r):
-        if topo.may_write(cores[e], cores[r]):
-            return cores[e]
-        return cores[e] + 2
+    v.memset(T.seed[:], 0.0).then_inc(sem.cs, 1)
+    v.wait_ge(sem.cs, 1)
+    for q in range(4):
+        v.memset(T.seed[32 * q:32 * q + 1, q:64:20], 1.0).then_inc(sem.cs, 1)
+        sl = [it[3] for it in wanted if it[6] == q and it[3] is not None]
+        v.memset(T.seed[32 * q:32 * q + 1, 64 + sl[0]:64 + sl[-1] + 1], 1.0).then_inc(sem.cs, 1)
+    pe.wait_ge(sem.cs, 9)
+    for m in range(4):
+        blk = T.seed[:, 16 * m:16 * m + 16]
+        pe.matmul(T.pc[0:16, 0:16], blk, blk, m == 0, m == 3).then_inc(sem.cm, 1)
+    pe.matmul(T.pc[0:16, 16:20], T.seed[:, 64:80], T.seed[:, 0:4], True, True).then_inc(sem.cm, 1)
+    v.wait_ge(sem.cm, 5)
+    v.tensor_copy(T.cst[:], T.pc[0:16, 0:20]).then_inc(sem.cc, 1)
+    ident, sel = T.cst[:, 0:16], T.cst[0:nrem, 16:20]
 
-    def nbits(m):
-        return bin(m).count("1")
+    pe.wait_ge(sem.cc, 1)
+    pe.wait_ge(sem.zl, 16)
+    for s in range(8):
+        pe.matmul(T.pz[0:zw, 16 * s:16 * s + 16], T.z3[:, zw * s:zw * s + zw], ident, True, True).then_inc(sem.zm, 1)
+    v.wait_ge(sem.zm, 8)
+    v.tensor_copy(T.zT[:], T.pz[0:zw, 0:128]).then_inc(sem.zc, 1)
+    sy.wait_ge(sem.zc, 1)
+    sy.dma_start(T.zd[0:nz], T.zT[0:nz, :]).then_inc(sem.zs, 16)
 
-    g.sync.dma_start(T.zs[:], T.z[:]).then_inc(T.sem.zl, 16)
-    g.scalar.dma_start(T.gs[:], T.g[:]).then_inc(T.sem.gl, 16)
+    gsrc, ngv = T.g3, 0
+    if own:
+        gsrc = T.gp
+        v.memset(T.own[:], 0.0).then_inc(sem.gv, 1)
+        v.wait_ge(sem.gv, 1)
+        v.wait_ge(sem.gl, 16)
+        v.wait_ge(sem.zl, 16)
+        ngv = 1
+        for it in own:
+            j = it[6] * nk + it[7]
+            v.tensor_tensor(T.own[:, it[6]:32:nt], T.z3[:, it[1]:8 * zw:zw], T.g3[:, :, j], AluOpType.mult).then_inc(
+                sem.gv, 1)
+            ngv += 1
+        cuts = [-1] + [it[6] * nk + it[7] for it in own] + [nt * nk]
+        for n in range(len(cuts) - 1):
+            lo, hi = cuts[n] + 1, cuts[n + 1]
+            if lo < hi:
+                v.tensor_copy(T.gp[:, :, lo - n:hi - n], T.g3[:, :, lo:hi]).then_inc(sem.gv, 1)
+                ngv += 1
+        pe.wait_ge(sem.gv, ngv)
+    pe.wait_ge(sem.gl, 16)
+    for s in range(8):
+        pe.matmul(T.pg[0:nrem, 16 * s:16 * s + 16], gsrc[:, s, 0:nrem], ident, True, True).then_inc(sem.gm, 1)
 
-    sent = 0
-    g.wait_ge(T.sem.zl, 16)
-    needs_relay = any(block(me, r)[1] and carrier(me, r) != core for r in range(n) if r != me)
-    if needs_relay:
-        rid, pid, _ = topo.addr(core + 2)
-        m = topo.mask(core, core + 2)
-        g.remote_dma(T.rz[:], T.zs[:], T.sem.relay, T.sem.sent, pid, rid, m)
-        sent += nbits(m)
-    for r in range(n):
-        o, c = block(me, r)
-        if r == me or not c or carrier(me, r) != core:
-            continue
-        rid, pid, _ = topo.addr(cores[r])
-        m = topo.mask(core, cores[r])
-        s = slot(r, me)
-        g.remote_dma(T.land[:, s:s + c], T.zs[:, o:o + c], T.sem.arrived, T.sem.sent, pid, rid, m)
-        sent += nbits(m)
-    if core % 4 >= 2:
-        e = me - 2
-        fw = [r for r in range(n) if block(e, r)[1] and carrier(e, r) == core]
-        if fw:
-            g.wait_ge(T.sem.relay, 16)
-        for r in fw:
-            o, c = block(e, r)
-            rid, pid, _ = topo.addr(cores[r])
-            m = topo.mask(core, cores[r])
-            s = slot(r, e)
-            g.remote_dma(T.land[:, s:s + c], T.rz[:, o:o + c], T.sem.arrived, T.sem.sent, pid, rid, m)
-            sent += nbits(m)
-    g.wait_ge(T.sem.sent, sent)
+    first = [(it[4], T.rl[it[5]], T.zd[it[1]], sem.relay) for it in mine if it[4] is not None]
+    direct = [(it[2], T.land[it[3]], T.zd[it[1]], sem.arrived) for it in mine if it[4] is None and it[3] is not None]
+    g.wait_ge(sem.zs, 16)
+    emit(first + direct)
+    pass_on()
 
-    expect = 0
-    for e in range(n):
-        if e != me and block(e, me)[1]:
-            expect += nbits(topo.mask(carrier(e, me), core))
-    v = g.vector
-    v.wait_ge(T.sem.gl, 16)
-    v.wait_ge(T.sem.zl, 16)
-    v.wait_ge(T.sem.arrived, expect)
-    for t in range(nt):
-        for k in range(nk):
-            e = route[me][t][k]
-            i = col[e].index((me, t, k))
-            if e == me:
-                src = T.zs[:, i:i + 1]
-            else:
-                p = slot(me, e) + i - block(e, me)[0]
-                src = T.land[:, p:p + 1]
-            q = k * nt + t
-            v.tensor_tensor(T.prod[:, q:q + 1], T.gs[:, t * nk + k:t * nk + k + 1], src, AluOpType.mult).then_inc(T.sem.vs, 1)
-    v.wait_ge(T.sem.vs, 16)
-    v.tensor_tensor(T.half[:], T.prod[:, 0:8], T.prod[:, 8:16], AluOpType.add).then_inc(T.sem.vs, 1)
-    v.wait_ge(T.sem.vs, 17)
-    v.tensor_tensor(T.ys[:], T.half[:, 0:4], T.half[:, 4:8], AluOpType.add).then_inc(T.sem.vs, 1)
-    g.sync.wait_ge(T.sem.vs, 18)
-    g.sync.dma_start(T.y[:], T.ys[:]).then_inc(T.sem.stored, 16)
-    g.sync.wait_ge(T.sem.stored, 16)
+    sy.wait_ge(sem.arrived, nrem)
+    sy.dma_start(T.lt[0:nrem, :], T.land[0:nrem]).then_inc(sem.ll, 16)
+    v.wait_ge(sem.ll, 16)
+    v.wait_ge(sem.gm, 8)
+    v.tensor_tensor(T.prod[0:nrem, :], T.lt[0:nrem, :], T.pg[0:nrem, 0:128], AluOpType.mult).then_inc(sem.pm, 1)
+    pe.wait_ge(sem.pm, 1)
+    for s in range(8):
+        pe.matmul(T.py[0:16, nt * s:nt * s + nt], T.prod[0:nrem, 16 * s:16 * s + 16], sel, True, True).then_inc(sem.ym, 1)
+    v.wait_ge(sem.ym, 8)
+    if own:
+        v.wait_ge(sem.gv, ngv)
+        v.tensor_tensor(T.y3[:], T.py[0:16, 0:32], T.own[:], AluOpType.add).then_inc(sem.yc, 1)
+    else:
+        v.tensor_copy(T.y3[:], T.py[0:16, 0:32]).then_inc(sem.yc, 1)
+    sy.wait_ge(sem.yc, 1)
+    sy.dma_start(T.y[:], T.y3[:]).then_inc(sem.st, 16)
+    sy.wait_ge(sem.st, 16)

from concourse.bass import DstId, RemoteDMATransfer
from concourse.mybir import AluOpType

RMAX = 32
SCRATCH = {
    "z3": ("sbuf", [16, 168], "float32"),
    "g3": ("sbuf", [16, 8, 16], "float32"),
    "gp": ("sbuf", [16, 8, 16], "float32"),
    "seed": ("sbuf", [128, 80], "float32"),
    "cst": ("sbuf", [16, 20], "float32"),
    "zT": ("sbuf", [21, 128], "float32"),
    "lt": ("sbuf", [16, 128], "float32"),
    "prod": ("sbuf", [16, 128], "float32"),
    "own": ("sbuf", [16, 32], "float32"),
    "y3": ("sbuf", [16, 32], "float32"),
    "zd": ("dram", [21, 128, 1], "float32"),
    "land": ("dram", [16, 128, 1], "float32"),
    "rl": ("dram", [RMAX, 128, 1], "float32"),
    "pc": ("psum", [128, 512], "float32"),
    "pz": ("psum", [128, 512], "float32"),
    "pg": ("psum", [128, 512], "float32"),
    "py": ("psum", [128, 512], "float32"),
}
SEMAPHORES = ["zl", "gl", "cs", "cm", "cc", "zm", "zc", "zs", "gv", "gm", "arrived", "relay", "sent", "ll", "pm", "ym",
              "yc", "st"]

CACHE = {}


def links(topo, s, d):
    a, b = topo.chip(s), topo.chip(d)
    out = [("w", s), ("l", d)]
    if a != b:
        dd = topo.die(s)
        out += [("out", a), ("in", b)]
        if (a & 1) != (b & 1):
            out.append(("mate", a, dd))
            a ^= 1
        if a != b:
            out += [("so", a, dd), ("si", b, dd)]
    return out


def plan(T, topo):
    if "plan" in CACHE:
        return CACHE["plan"]
    cores = T.cores
    route = T.tables["ROUTE"]
    fill = [0] * len(cores)
    raw = []
    for r, toks in enumerate(route):
        slot = 0
        for t, exps in enumerate(toks):
            for k, e in enumerate(exps):
                raw.append([cores[e], fill[e], cores[r], None if e == r else slot, None, None, t, k])
                fill[e] += 1
                slot += e != r

    ncore = (max(cores) // 8 + 1) * 8
    pw = [n ** 6 for n in range(len(raw) * 2 + 2)]
    weight = {"w": 4096, "l": 4096, "mate": 4096, "so": 4096, "si": 4096, "out": 1, "in": 1}
    load = {}

    def way(it, q):
        return links(topo, it[0], it[2]) if q is None else links(topo, it[0], q) + links(topo, q, it[2])

    def put(ks, sign):
        cost = 0
        for key in ks:
            n = load.get(key, 0)
            cost += weight[key[0]] * (pw[n + sign] - pw[n])
            load[key] = n + sign
        return cost

    ways = []
    for it in raw:
        src, dst = it[0], it[2]
        if src == dst:
            ways.append([])
            continue
        opts = [None] if topo.may_write(src, dst) else []
        if (topo.chip(src) & 1) != (topo.chip(dst) & 1):
            opts += [q for q in range(ncore) if q != src and (topo.chip(q) & 1) == (topo.chip(src) & 1)
                     and topo.may_write(q, dst)]
        ways.append([(q, way(it, q)) for q in opts])
    chosen = [None] * len(raw)
    for sweep in range(16):
        moved = False
        for i, opts in enumerate(ways):
            if not opts or (sweep and len(opts) < 2):
                continue
            if chosen[i] is not None:
                put(chosen[i][1], -1)
            best = None
            for o in opts:
                cost = put(o[1], 1)
                put(o[1], -1)
                if best is None or cost < best[0]:
                    best = (cost, o)
            moved = moved or best[1] is not chosen[i]
            chosen[i] = best[1]
            put(best[1][1], 1)
        if not moved:
            break

    res = {"src": {}, "via": {}, "dst": {}}
    for it, ch in zip(raw, chosen):
        if ch is not None and ch[0] is not None:
            it[4] = ch[0]
            it[5] = len(res["via"].setdefault(ch[0], []))
            assert it[5] < RMAX
            res["via"][ch[0]].append(it)
        res["src"].setdefault(it[0], []).append(it)
        res["dst"].setdefault(it[2], []).append(it)
    CACHE["plan"] = res
    return res


def rank_program(g, core, T, topo):
    routes = plan(T, topo)
    sem = T.sem
    thru = routes["via"].get(core, [])
    nsent = [0]

    def emit(writes):
        todo = list(writes)
        while todo:
            far = [w for w in todo if topo.chip(w[0]) != topo.chip(core)][:8]
            near = [w for w in todo if topo.chip(w[0]) == topo.chip(core)][:16 - len(far)]
            call = []
            for eng, w in enumerate(far + near):
                rid, pid, _ = topo.addr(w[0])
                call.append(RemoteDMATransfer(dst_ids=[DstId(rid=rid, pnc=pid)], dma_engine_mask=1 << eng,
                                              remote_sem=w[3], src=w[2], dst=w[1]))
                todo.remove(w)
            g.remote_dma_fused(call, local_sem=sem.sent)
            nsent[0] += len(call)

    def pass_on():
        if thru:
            g.wait_ge(sem.relay, len(thru))
            emit([(it[2], T.land[it[3]], T.rl[it[5]], sem.arrived) for it in thru])
        if nsent[0]:
            g.wait_ge(sem.sent, nsent[0])

    if T.rank_of(core) is None:
        pass_on()
        return

    nt, nk, zw = T.tables["T"], T.tables["K"], T.tables["ZW"]
    assert nt == 4 and nk == 4 and zw == 21
    v, pe, sy, sc = g.vector, g.tensor, g.sync, g.scalar
    mine = routes["src"].get(core, [])
    wanted = routes["dst"][core]
    own = [it for it in wanted if it[3] is None]
    nz, nrem = len(mine), len(wanted) - len(own)

    sy.dma_start(T.z3[:], T.z[:]).then_inc(sem.zl, 16)
    sc.dma_start(T.g3[:], T.g[:]).then_inc(sem.gl, 16)

    v.memset(T.seed[:], 0.0).then_inc(sem.cs, 1)
    v.wait_ge(sem.cs, 1)
    for q in range(4):
        v.memset(T.seed[32 * q:32 * q + 1, q:64:20], 1.0).then_inc(sem.cs, 1)
        sl = [it[3] for it in wanted if it[6] == q and it[3] is not None]
        v.memset(T.seed[32 * q:32 * q + 1, 64 + sl[0]:64 + sl[-1] + 1], 1.0).then_inc(sem.cs, 1)
    pe.wait_ge(sem.cs, 9)
    for m in range(4):
        blk = T.seed[:, 16 * m:16 * m + 16]
        pe.matmul(T.pc[0:16, 0:16], blk, blk, m == 0, m == 3).then_inc(sem.cm, 1)
    pe.matmul(T.pc[0:16, 16:20], T.seed[:, 64:80], T.seed[:, 0:4], True, True).then_inc(sem.cm, 1)
    v.wait_ge(sem.cm, 5)
    v.tensor_copy(T.cst[:], T.pc[0:16, 0:20]).then_inc(sem.cc, 1)
    ident, sel = T.cst[:, 0:16], T.cst[0:nrem, 16:20]

    pe.wait_ge(sem.cc, 1)
    pe.wait_ge(sem.zl, 16)
    for s in range(8):
        pe.matmul(T.pz[0:zw, 16 * s:16 * s + 16], T.z3[:, zw * s:zw * s + zw], ident, True, True).then_inc(sem.zm, 1)
    v.wait_ge(sem.zm, 8)
    v.tensor_copy(T.zT[:], T.pz[0:zw, 0:128]).then_inc(sem.zc, 1)
    sy.wait_ge(sem.zc, 1)
    sy.dma_start(T.zd[0:nz], T.zT[0:nz, :]).then_inc(sem.zs, 16)

    gsrc, ngv = T.g3, 0
    if own:
        gsrc = T.gp
        v.memset(T.own[:], 0.0).then_inc(sem.gv, 1)
        v.wait_ge(sem.gv, 1)
        v.wait_ge(sem.gl, 16)
        v.wait_ge(sem.zl, 16)
        ngv = 1
        for it in own:
            j = it[6] * nk + it[7]
            v.tensor_tensor(T.own[:, it[6]:32:nt], T.z3[:, it[1]:8 * zw:zw], T.g3[:, :, j], AluOpType.mult).then_inc(
                sem.gv, 1)
            ngv += 1
        cuts = [-1] + [it[6] * nk + it[7] for it in own] + [nt * nk]
        for n in range(len(cuts) - 1):
            lo, hi = cuts[n] + 1, cuts[n + 1]
            if lo < hi:
                v.tensor_copy(T.gp[:, :, lo - n:hi - n], T.g3[:, :, lo:hi]).then_inc(sem.gv, 1)
                ngv += 1
        pe.wait_ge(sem.gv, ngv)
    pe.wait_ge(sem.gl, 16)
    for s in range(8):
        pe.matmul(T.pg[0:nrem, 16 * s:16 * s + 16], gsrc[:, s, 0:nrem], ident, True, True).then_inc(sem.gm, 1)

    first = [(it[4], T.rl[it[5]], T.zd[it[1]], sem.relay) for it in mine if it[4] is not None]
    direct = [(it[2], T.land[it[3]], T.zd[it[1]], sem.arrived) for it in mine if it[4] is None and it[3] is not None]
    g.wait_ge(sem.zs, 16)
    emit(first + direct)
    pass_on()

    sy.wait_ge(sem.arrived, nrem)
    sy.dma_start(T.lt[0:nrem, :], T.land[0:nrem]).then_inc(sem.ll, 16)
    v.wait_ge(sem.ll, 16)
    v.wait_ge(sem.gm, 8)
    v.tensor_tensor(T.prod[0:nrem, :], T.lt[0:nrem, :], T.pg[0:nrem, 0:128], AluOpType.mult).then_inc(sem.pm, 1)
    pe.wait_ge(sem.pm, 1)
    for s in range(8):
        pe.matmul(T.py[0:16, nt * s:nt * s + nt], T.prod[0:nrem, 16 * s:16 * s + 16], sel, True, True).then_inc(sem.ym, 1)
    v.wait_ge(sem.ym, 8)
    if own:
        v.wait_ge(sem.gv, ngv)
        v.tensor_tensor(T.y3[:], T.py[0:16, 0:32], T.own[:], AluOpType.add).then_inc(sem.yc, 1)
    else:
        v.tensor_copy(T.y3[:], T.py[0:16, 0:32]).then_inc(sem.yc, 1)
    sy.wait_ge(sem.yc, 1)
    sy.dma_start(T.y[:], T.y3[:]).then_inc(sem.st, 16)
    sy.wait_ge(sem.st, 16)
